import numpy as np
import ml_dtypes


def mxq(x, axis, fmt="e4m3"):
    dtype, down = {"e4m3": (ml_dtypes.float8_e4m3fn, 7), "e5m2": (ml_dtypes.float8_e5m2, 14)}[fmt]
    v = np.moveaxis(np.asarray(x, np.float32).astype(ml_dtypes.bfloat16).astype(np.float64), axis, -1)
    blocks = v.reshape(v.shape[:-1] + (-1, 32))
    amax = np.abs(blocks).max(-1, keepdims=True)
    byte = np.maximum(np.where(amax > 0, np.frexp(amax)[1] - 1 + 127, 0) - down, 1)
    scale = np.exp2(byte - 127.0)
    codes = (blocks / scale).astype(np.float32).astype(dtype).astype(np.float64)
    return np.moveaxis((codes * scale).reshape(v.shape), -1, axis)


WIDE = False


def mx_kscale(k):
    if not WIDE:
        return np.ones(k)
    levels = np.array([10, -10, 5, -5, 0])
    if k % 512:
        return np.exp2(np.random.permutation(np.resize(levels, k // 32))).repeat(32)
    a = np.empty((k // 512, 16))
    for p in range(k // 512):
        a[p, :8] = np.random.permutation(np.resize(levels, 8))
        for g in range(8):
            far = levels[np.abs(levels - a[p, g]) >= 10]
            a[p, g + 8] = far[np.random.randint(len(far))]
    return np.exp2(a.ravel()).repeat(32)


def f64(x):
    return np.asarray(x).astype(np.float64)


def striped(idx):
    return np.tile(idx.reshape(-1, 16).T, (8, 1)).astype(np.uint16)


def unstriped(offs):
    return offs[:16].T.reshape(-1).astype(np.int64)


def pack_weight(w):
    k, n = w.shape
    w = f64(np.asarray(w, np.float32).astype(ml_dtypes.bfloat16)).reshape(k // 32, 32, n)
    amax = np.abs(w).max(1)
    byte = np.clip(np.where(amax > 0, np.frexp(amax)[1] - 1 + 127 - 7, 1), 1, 254)
    scaled = (w * np.exp2(127.0 - byte)[:, None, :]).reshape(k, n).astype(np.float32)
    words = np.ascontiguousarray(scaled.reshape(k // 512, 128, 4, n).transpose(0, 1, 3, 2)).astype(ml_dtypes.float8_e4m3fn).view(np.uint8)
    return words, np.ascontiguousarray(byte.astype(np.uint8).reshape(k // 512, 16, n))


def unpack_weight(words, scales):
    g, p, n, _ = words.shape
    vals = np.ascontiguousarray(words).view(ml_dtypes.float8_e4m3fn).astype(np.float64) * np.repeat(np.exp2(scales.astype(np.float64) - 127.0), 8, axis=1)[..., None]
    return vals.transpose(0, 1, 3, 2).reshape(g * 512, n)


K, T, S, N = 512, 1024, 512, 128


def setup_inputs():
    n = np.random.standard_normal
    s = mx_kscale(K)[:, None]
    packed_xT = pack_weight(n((K, T)) * s)
    return {
        "x_words": packed_xT[0],
        "x_scales": packed_xT[1],
        "w1": (n((K, N)) / np.sqrt(K) / s).astype(np.float32),
        "mob": (np.random.uniform(0.05, 0.25, (N, 1))).astype(np.float32),
        "offs": striped(np.random.permutation(T)[:S]),
        "pos1": striped(np.random.permutation(S)[:S]),
        "pos2": striped(np.random.permutation(S)[:S]),
        "pos3": striped(np.random.permutation(S)[:S]),
    }


def reference(x_words, x_scales, w1, mob, offs, pos1, pos2, pos3):
    xq = unpack_weight(x_words, x_scales)[:, unstriped(offs)]
    y = mxq(f64(w1), 0, "e4m3").T @ xq
    con = np.tanh(y)
    mu = con * ((con) ** 2 - 1.0) - (0.2 * (con[:, unstriped(pos1)] + con[:, unstriped(pos2)] + con[:, unstriped(pos3)] - (3.0 * con)))
    return con + f64(mob) * (mu[:, unstriped(pos1)] + mu[:, unstriped(pos2)] + mu[:, unstriped(pos3)] - (3.0 * mu))

@@ -1,0 +1,119 @@
+import math
+from contextlib import ExitStack
+
+import concourse.mybir as mybir
+
+F32 = mybir.dt.float32
+BF16 = mybir.dt.bfloat16
+I32 = mybir.dt.int32
+U32 = mybir.dt.uint32
+U16 = mybir.dt.uint16
+U8 = mybir.dt.uint8
+FP8X4 = mybir.dt.float8_e4m3fn_x4
+ACT = mybir.ActivationFunctionType
+ALU = mybir.AluOpType
+
+P = 128
+K, T, S, N = 512, 1024, 512, 128
+HALF = S // 2
+FLOPS = 2 * K * N * S
+
+
+def tile_picked_ycahnh_cub_p_kernel(tc, x_words, x_scales, w1, mob, offs, pos1, pos2, pos3, out):
+    nc = tc.nc
+    with ExitStack() as ctx:
+        keep = ctx.enter_context(tc.tile_pool(name="keep", bufs=1))
+        psum = ctx.enter_context(tc.psum_pool(name="psum", bufs=1))
+
+        offs_t = keep.tile([P, S // 16], U16, name="offs_t")
+        p1 = keep.tile([P, S // 16], U16, name="p1")
+        p2 = keep.tile([P, S // 16], U16, name="p2")
+        p3 = keep.tile([P, S // 16], U16, name="p3")
+        xw = keep.tile([P, T], I32, name="xw", align_bytes=64)
+        xs = keep.tile([P, T], U8, name="xs", align_bytes=64)
+        wraw = keep.tile([P, 4, N], F32, name="wraw", align_bytes=64)
+        mob_t = keep.tile([P, 1], F32, name="mob_t")
+        warm_in = keep.tile([P, 1], F32, name="warm_in")
+        warm_out = keep.tile([P, 1], F32, name="warm_out")
+
+        nc.sync.dma_start(offs_t[:], offs)
+        for q in range(4):
+            rows = x_scales[0, 4 * q : 4 * q + 4, :].bitcast(I32)
+            queue = nc.sync if q < 2 else nc.scalar
+            queue.dma_start(xs[32 * q : 32 * q + 32, :].bitcast(I32), rows.unsqueeze(0).to_broadcast([8, 4, T // 4]))
+        nc.sync.dma_start(wraw[:], w1.rearrange("(p j) m -> p j m", j=4))
+        nc.sync.dma_start(xw[:], x_words[0].rearrange("p n t -> p (n t)").bitcast(I32))
+        nc.vector.memset(warm_in[:], 0.0)
+        nc.scalar.activation(warm_out[:], warm_in[:], ACT.Sigmoid)
+        nc.sync.dma_start(p3[:], pos3)
+        nc.sync.dma_start(p1[:], pos1)
+        nc.sync.dma_start(p2[:], pos2)
+        nc.sync.dma_start(mob_t[:], mob)
+
+        def lst(t, c):
+            return t[:, c.start // 16 : c.stop // 16]
+
+        H = [slice(0, 256), slice(256, 512)]
+        X, Y, Z = slice(0, 256), slice(256, 384), slice(384, 512)
+
+        gs = keep.tile([P, S], U8, name="gs", align_bytes=64)
+        nc.vector.tensor_copy(gs[:], xs[:].indirect(offs_t[:]))
+
+        wbf = keep.tile([P, N, 4], BF16, name="wbf", align_bytes=64)
+        nc.scalar.copy(wbf[:], wraw[:].rearrange("p j m -> p m j"))
+        wq = keep.tile([P, N], U32, name="wq", align_bytes=64)
+        wsc = keep.tile([P, N], U8, name="wsc", align_bytes=64)
+        kap = keep.tile([P, 1], F32, name="kap")
+        nc.vector.quantize_mx(out=wq[:].bitcast(FP8X4), scales=wsc[:], in_=wbf[:].rearrange("p m j -> p (m j)"))
+
+        gw = keep.tile([P, S], U32, name="gw", align_bytes=64)
+        y2 = keep.tile([P, S], F32, name="y2")
+        con = keep.tile([P, S], F32, name="con")
+        sq = keep.tile([P, S], F32, name="sq")
+        ne = keep.tile([P, S], F32, name="ne")
+        banks = []
+        for i, c in enumerate((X, Y, Z)):
+            nc.vector.tensor_copy(gw[:, c], xw[:].bitcast(U32).indirect(lst(offs_t, c)))
+            bank = psum.tile([P, c.stop - c.start], F32, name=f"bank{i}")
+            nc.tensor.matmul_mx(out=bank[:], lhsT=wq[:].bitcast(FP8X4), lhsT_scale=wsc[:],
+                                rhs=gw[:, c].bitcast(FP8X4), rhs_scale=gs[:, c], start=True, stop=True)
+            banks.append(bank)
+        s1 = keep.tile([P, S], F32, name="s1")
+        s2 = keep.tile([P, S], F32, name="s2")
+        a = keep.tile([P, S], F32, name="a")
+        b = keep.tile([P, S], F32, name="b")
+        c = keep.tile([P, S], F32, name="c")
+        n3 = keep.tile([P, S], F32, name="n3")
+        nc.scalar.mul(kap[:], mob_t[:], -0.2)
+        for i, c_ in enumerate((X, Y, Z)):
+            nc.scalar.activation(con[:, c_], banks[i][:], ACT.Tanh)
+            nc.vector.tensor_scalar(y2[:, c_], banks[i][:], 2.0, None, ALU.mult)
+        for h in H:
+            nc.scalar.activation(sq[:, h], con[:, h], ACT.Square, scale=math.sqrt(5.0))
+        for h in H:
+            nc.scalar.activation(s1[:, h], y2[:].indirect(lst(p1, h)), ACT.Sigmoid)
+        for h in H:
+            nc.scalar.activation(s2[:, h], y2[:].indirect(lst(p2, h)), ACT.Sigmoid)
+        for h in H:
+            nc.vector.scalar_tensor_tensor(ne[:, h], sq[:, h], 2.0, con[:, h], ALU.subtract, ALU.mult)
+        for h in H:
+            nc.vector.tensor_tensor(a[:, h], con[:].indirect(lst(p3, h)), ne[:, h], ALU.subtract)
+        for h in H:
+            nc.vector.scalar_tensor_tensor(b[:, h], s1[:, h], 2.0, a[:, h], ALU.mult, ALU.add)
+        for h in H:
+            nc.vector.scalar_tensor_tensor(c[:, h], s2[:, h], 2.0, b[:, h], ALU.mult, ALU.add)
+            nc.scalar.activation(n3[:, h], c[:, h], ACT.Copy, scale=-3.0)
+
+        t1 = keep.tile([P, S], F32, name="t1")
+        t2 = keep.tile([P, S], F32, name="t2")
+        t3 = keep.tile([P, S], F32, name="t3")
+        res = keep.tile([P, S], F32, name="res")
+        for h in H:
+            nc.vector.tensor_tensor(t1[:, h], c[:].indirect(lst(p1, h)), n3[:, h], ALU.add)
+        for h in H:
+            nc.vector.tensor_tensor(t2[:, h], c[:].indirect(lst(p2, h)), t1[:, h], ALU.add)
+        for h in H:
+            nc.vector.tensor_tensor(t3[:, h], c[:].indirect(lst(p3, h)), t2[:, h], ALU.add)
+        for h in H:
+            nc.vector.scalar_tensor_tensor(res[:, h], t3[:, h], kap[:], con[:, h], ALU.mult, ALU.add)
+            nc.sync.dma_start(out[:, h], res[:, h])

@@ -15,7 +15,6 @@ ALU = mybir.AluOpType
 
 P = 128
 K, T, S, N = 512, 1024, 512, 128
-HALF = S // 2
 FLOPS = 2 * K * N * S
 
 
@@ -43,18 +42,18 @@ def tile_picked_ycahnh_cub_p_kernel(tc, x_words, x_scales, w1, mob, offs, pos1, 
             queue.dma_start(xs[32 * q : 32 * q + 32, :].bitcast(I32), rows.unsqueeze(0).to_broadcast([8, 4, T // 4]))
         nc.sync.dma_start(wraw[:], w1.rearrange("(p j) m -> p j m", j=4))
         nc.sync.dma_start(xw[:], x_words[0].rearrange("p n t -> p (n t)").bitcast(I32))
+        nc.sync.dma_start(mob_t[:], mob)
         nc.vector.memset(warm_in[:], 0.0)
         nc.scalar.activation(warm_out[:], warm_in[:], ACT.Sigmoid)
         nc.sync.dma_start(p3[:], pos3)
         nc.sync.dma_start(p1[:], pos1)
         nc.sync.dma_start(p2[:], pos2)
-        nc.sync.dma_start(mob_t[:], mob)
 
         def lst(t, c):
             return t[:, c.start // 16 : c.stop // 16]
 
         H = [slice(0, 256), slice(256, 512)]
-        X, Y, Z = slice(0, 256), slice(256, 384), slice(384, 512)
+        Q = [slice(128 * i, 128 * (i + 1)) for i in range(4)]
 
         gs = keep.tile([P, S], U8, name="gs", align_bytes=64)
         nc.vector.tensor_copy(gs[:], xs[:].indirect(offs_t[:]))
@@ -63,57 +62,95 @@ def tile_picked_ycahnh_cub_p_kernel(tc, x_words, x_scales, w1, mob, offs, pos1, 
         nc.scalar.copy(wbf[:], wraw[:].rearrange("p j m -> p m j"))
         wq = keep.tile([P, N], U32, name="wq", align_bytes=64)
         wsc = keep.tile([P, N], U8, name="wsc", align_bytes=64)
-        kap = keep.tile([P, 1], F32, name="kap")
+        kap2 = keep.tile([P, 1], F32, name="kap2")
+        nc.scalar.mul(kap2[:], mob_t[:], -0.4)
         nc.vector.quantize_mx(out=wq[:].bitcast(FP8X4), scales=wsc[:], in_=wbf[:].rearrange("p m j -> p (m j)"))
 
         gw = keep.tile([P, S], U32, name="gw", align_bytes=64)
-        y2 = keep.tile([P, S], F32, name="y2")
-        con = keep.tile([P, S], F32, name="con")
-        sq = keep.tile([P, S], F32, name="sq")
-        ne = keep.tile([P, S], F32, name="ne")
+        names = ["y2", "con", "sq", "ne", "wc", "s1", "s2", "a", "b", "mu", "base", "t1", "t2", "t3"]
+        y2, con, sq, ne, wc, s1, s2, a, b, mu, base, t1, t2, t3 = [keep.tile([P, S], F32, name=n) for n in names]
         banks = []
-        for i, c in enumerate((X, Y, Z)):
+        for i, c in enumerate(Q):
             nc.vector.tensor_copy(gw[:, c], xw[:].bitcast(U32).indirect(lst(offs_t, c)))
-            bank = psum.tile([P, c.stop - c.start], F32, name=f"bank{i}")
+            bank = psum.tile([P, 128], F32, name=f"bank{i}")
             nc.tensor.matmul_mx(out=bank[:], lhsT=wq[:].bitcast(FP8X4), lhsT_scale=wsc[:],
                                 rhs=gw[:, c].bitcast(FP8X4), rhs_scale=gs[:, c], start=True, stop=True)
             banks.append(bank)
-        s1 = keep.tile([P, S], F32, name="s1")
-        s2 = keep.tile([P, S], F32, name="s2")
-        a = keep.tile([P, S], F32, name="a")
-        b = keep.tile([P, S], F32, name="b")
-        c = keep.tile([P, S], F32, name="c")
-        n3 = keep.tile([P, S], F32, name="n3")
-        nc.scalar.mul(kap[:], mob_t[:], -0.2)
-        for i, c_ in enumerate((X, Y, Z)):
-            nc.scalar.activation(con[:, c_], banks[i][:], ACT.Tanh)
-            nc.vector.tensor_scalar(y2[:, c_], banks[i][:], 2.0, None, ALU.mult)
-        for h in H:
-            nc.scalar.activation(sq[:, h], con[:, h], ACT.Square, scale=math.sqrt(5.0))
-        for h in H:
-            nc.scalar.activation(s1[:, h], y2[:].indirect(lst(p1, h)), ACT.Sigmoid)
-        for h in H:
-            nc.scalar.activation(s2[:, h], y2[:].indirect(lst(p2, h)), ACT.Sigmoid)
-        for h in H:
-            nc.vector.scalar_tensor_tensor(ne[:, h], sq[:, h], 2.0, con[:, h], ALU.subtract, ALU.mult)
-        for h in H:
-            nc.vector.tensor_tensor(a[:, h], con[:].indirect(lst(p3, h)), ne[:, h], ALU.subtract)
-        for h in H:
-            nc.vector.scalar_tensor_tensor(b[:, h], s1[:, h], 2.0, a[:, h], ALU.mult, ALU.add)
-        for h in H:
-            nc.vector.scalar_tensor_tensor(c[:, h], s2[:, h], 2.0, b[:, h], ALU.mult, ALU.add)
-            nc.scalar.activation(n3[:, h], c[:, h], ACT.Copy, scale=-3.0)
 
-        t1 = keep.tile([P, S], F32, name="t1")
-        t2 = keep.tile([P, S], F32, name="t2")
-        t3 = keep.tile([P, S], F32, name="t3")
-        res = keep.tile([P, S], F32, name="res")
-        for h in H:
-            nc.vector.tensor_tensor(t1[:, h], c[:].indirect(lst(p1, h)), n3[:, h], ALU.add)
-        for h in H:
-            nc.vector.tensor_tensor(t2[:, h], c[:].indirect(lst(p2, h)), t1[:, h], ALU.add)
-        for h in H:
-            nc.vector.tensor_tensor(t3[:, h], c[:].indirect(lst(p3, h)), t2[:, h], ALU.add)
-        for h in H:
-            nc.vector.scalar_tensor_tensor(res[:, h], t3[:, h], kap[:], con[:, h], ALU.mult, ALU.add)
-            nc.sync.dma_start(out[:, h], res[:, h])
+        def tanh(i):
+            nc.scalar.activation(con[:, Q[i]], banks[i][:], ACT.Tanh)
+
+        def dbl_v(i):
+            nc.vector.tensor_scalar(y2[:, Q[i]], banks[i][:], 2.0, None, ALU.mult)
+
+        def dbl_a(i):
+            nc.scalar.activation(y2[:, Q[i]], banks[i][:], ACT.Copy, scale=2.0)
+
+        def square(c):
+            nc.scalar.activation(sq[:, c], con[:, c], ACT.Square, scale=math.sqrt(5.0))
+
+        def square_v(c):
+            nc.vector.scalar_tensor_tensor(sq[:, c], con[:, c], 5.0, con[:, c], ALU.mult, ALU.mult)
+
+        def scaled(c):
+            nc.vector.tensor_scalar(wc[:, c], con[:, c], mob_t[:], -0.2, ALU.mult, ALU.mult)
+
+        def well(c):
+            nc.vector.scalar_tensor_tensor(ne[:, c], sq[:, c], 2.0, wc[:, c], ALU.subtract, ALU.mult)
+
+        def sig(dst, p, c):
+            nc.scalar.activation(dst[:, c], y2[:].indirect(lst(p, c)), ACT.Sigmoid)
+
+        def third(c):
+            nc.vector.tensor_tensor(a[:, c], wc[:].indirect(lst(p3, c)), ne[:, c], ALU.subtract)
+
+        def addsig(dst, s, src, c):
+            nc.vector.scalar_tensor_tensor(dst[:, c], s[:, c], kap2[:], src[:, c], ALU.mult, ALU.add)
+
+        def mkbase(c):
+            nc.vector.scalar_tensor_tensor(base[:, c], mu[:, c], -3.0, con[:, c], ALU.mult, ALU.add)
+
+        def fetch(dst, p, src, c):
+            nc.vector.tensor_tensor(dst[:, c], mu[:].indirect(lst(p, c)), src[:, c], ALU.add)
+
+        tanh(0)
+        dbl_v(0)
+        tanh(1)
+        dbl_v(1)
+        square(Q[0])
+        tanh(2)
+        scaled(H[0])
+        square(Q[1])
+        dbl_v(2)
+        scaled(Q[2])
+        square_v(Q[2])
+        tanh(3)
+        dbl_a(3)
+        square(Q[3])
+        well(Q[2])
+        scaled(Q[3])
+        well(H[0])
+        well(Q[3])
+        sig(s1, p1, H[0])
+        sig(s1, p1, H[1])
+        sig(s2, p2, H[0])
+        sig(s2, p2, H[1])
+        third(H[0])
+        third(H[1])
+        addsig(b, s1, a, H[0])
+        addsig(b, s1, a, H[1])
+        addsig(mu, s2, b, H[0])
+        addsig(mu, s2, b, H[1])
+        mkbase(H[0])
+        fetch(t1, p1, base, H[0])
+        mkbase(H[1])
+        fetch(t2, p2, t1, H[0])
+        fetch(t1, p1, base, H[1])
+        fetch(t3, p3, t2, H[0])
+        nc.sync.dma_start(out[:, H[0]], t3[:, H[0]])
+        fetch(t2, p2, t1, Q[2])
+        fetch(t2, p2, t1, Q[3])
+        fetch(t3, p3, t2, Q[2])
+        nc.sync.dma_start(out[:, Q[2]], t3[:, Q[2]])
+        fetch(t3, p3, t2, Q[3])
+        nc.sync.dma_start(out[:, Q[3]], t3[:, Q[3]])

@@ -142,15 +142,9 @@ def tile_picked_ycahnh_cub_p_kernel(tc, x_words, x_scales, w1, mob, offs, pos1, 
         addsig(mu, s2, b, H[0])
         addsig(mu, s2, b, H[1])
         mkbase(H[0])
-        fetch(t1, p1, base, H[0])
         mkbase(H[1])
-        fetch(t2, p2, t1, H[0])
-        fetch(t1, p1, base, H[1])
-        fetch(t3, p3, t2, H[0])
-        nc.sync.dma_start(out[:, H[0]], t3[:, H[0]])
-        fetch(t2, p2, t1, Q[2])
-        fetch(t2, p2, t1, Q[3])
-        fetch(t3, p3, t2, Q[2])
-        nc.sync.dma_start(out[:, Q[2]], t3[:, Q[2]])
-        fetch(t3, p3, t2, Q[3])
-        nc.sync.dma_start(out[:, Q[3]], t3[:, Q[3]])
+        for dst, p, src in ((t1, p1, base), (t2, p2, t1), (t3, p3, t2)):
+            for h in H:
+                fetch(dst, p, src, h)
+        for h in H:
+            nc.sync.dma_start(out[:, h], t3[:, h])

import math
from contextlib import ExitStack

import concourse.mybir as mybir

F32 = mybir.dt.float32
BF16 = mybir.dt.bfloat16
I32 = mybir.dt.int32
U32 = mybir.dt.uint32
U16 = mybir.dt.uint16
U8 = mybir.dt.uint8
FP8X4 = mybir.dt.float8_e4m3fn_x4
ACT = mybir.ActivationFunctionType
ALU = mybir.AluOpType

P = 128
K, T, S, N = 512, 1024, 512, 128
FLOPS = 2 * K * N * S


def tile_picked_ycahnh_cub_p_kernel(tc, x_words, x_scales, w1, mob, offs, pos1, pos2, pos3, out):
    nc = tc.nc
    with ExitStack() as ctx:
        keep = ctx.enter_context(tc.tile_pool(name="keep", bufs=1))
        psum = ctx.enter_context(tc.psum_pool(name="psum", bufs=1))

        offs_t = keep.tile([P, S // 16], U16, name="offs_t")
        p1 = keep.tile([P, S // 16], U16, name="p1")
        p2 = keep.tile([P, S // 16], U16, name="p2")
        p3 = keep.tile([P, S // 16], U16, name="p3")
        xw = keep.tile([P, T], I32, name="xw", align_bytes=64)
        xs = keep.tile([P, T], U8, name="xs", align_bytes=64)
        wraw = keep.tile([P, 4, N], F32, name="wraw", align_bytes=64)
        mob_t = keep.tile([P, 1], F32, name="mob_t")
        warm_in = keep.tile([P, 1], F32, name="warm_in")
        warm_out = keep.tile([P, 1], F32, name="warm_out")

        nc.sync.dma_start(offs_t[:], offs)
        for q in range(4):
            rows = x_scales[0, 4 * q : 4 * q + 4, :].bitcast(I32)
            queue = nc.sync if q < 2 else nc.scalar
            queue.dma_start(xs[32 * q : 32 * q + 32, :].bitcast(I32), rows.unsqueeze(0).to_broadcast([8, 4, T // 4]))
        nc.sync.dma_start(wraw[:], w1.rearrange("(p j) m -> p j m", j=4))
        nc.sync.dma_start(xw[:], x_words[0].rearrange("p n t -> p (n t)").bitcast(I32))
        nc.sync.dma_start(mob_t[:], mob)
        nc.vector.memset(warm_in[:], 0.0)
        nc.scalar.activation(warm_out[:], warm_in[:], ACT.Sigmoid)
        nc.sync.dma_start(p3[:], pos3)
        nc.sync.dma_start(p1[:], pos1)
        nc.sync.dma_start(p2[:], pos2)

        def lst(t, c):
            return t[:, c.start // 16 : c.stop // 16]

        H = [slice(0, 256), slice(256, 512)]
        Q = [slice(128 * i, 128 * (i + 1)) for i in range(4)]

        gs = keep.tile([P, S], U8, name="gs", align_bytes=64)
        nc.vector.tensor_copy(gs[:], xs[:].indirect(offs_t[:]))

        wbf = keep.tile([P, N, 4], BF16, name="wbf", align_bytes=64)
        nc.scalar.copy(wbf[:], wraw[:].rearrange("p j m -> p m j"))
        wq = keep.tile([P, N], U32, name="wq", align_bytes=64)
        wsc = keep.tile([P, N], U8, name="wsc", align_bytes=64)
        kap2 = keep.tile([P, 1], F32, name="kap2")
        nc.scalar.mul(kap2[:], mob_t[:], -0.4)
        nc.vector.quantize_mx(out=wq[:].bitcast(FP8X4), scales=wsc[:], in_=wbf[:].rearrange("p m j -> p (m j)"))

        gw = keep.tile([P, S], U32, name="gw", align_bytes=64)
        names = ["y2", "con", "sq", "ne", "wc", "s1", "s2", "a", "b", "mu", "base", "t1", "t2", "t3"]
        y2, con, sq, ne, wc, s1, s2, a, b, mu, base, t1, t2, t3 = [keep.tile([P, S], F32, name=n) for n in names]
        banks = []
        for i, c in enumerate(Q):
            nc.vector.tensor_copy(gw[:, c], xw[:].bitcast(U32).indirect(lst(offs_t, c)))
            bank = psum.tile([P, 128], F32, name=f"bank{i}")
            nc.tensor.matmul_mx(out=bank[:], lhsT=wq[:].bitcast(FP8X4), lhsT_scale=wsc[:],
                                rhs=gw[:, c].bitcast(FP8X4), rhs_scale=gs[:, c], start=True, stop=True)
            banks.append(bank)

        def tanh(i):
            nc.scalar.activation(con[:, Q[i]], banks[i][:], ACT.Tanh)

        def dbl_v(i):
            nc.vector.tensor_scalar(y2[:, Q[i]], banks[i][:], 2.0, None, ALU.mult)

        def dbl_a(i):
            nc.scalar.activation(y2[:, Q[i]], banks[i][:], ACT.Copy, scale=2.0)

        def square(c):
            nc.scalar.activation(sq[:, c], con[:, c], ACT.Square, scale=math.sqrt(5.0))

        def square_v(c):
            nc.vector.scalar_tensor_tensor(sq[:, c], con[:, c], 5.0, con[:, c], ALU.mult, ALU.mult)

        def scaled(c):
            nc.vector.tensor_scalar(wc[:, c], con[:, c], mob_t[:], -0.2, ALU.mult, ALU.mult)

        def well(c):
            nc.vector.scalar_tensor_tensor(ne[:, c], sq[:, c], 2.0, wc[:, c], ALU.subtract, ALU.mult)

        def sig(dst, p, c):
            nc.scalar.activation(dst[:, c], y2[:].indirect(lst(p, c)), ACT.Sigmoid)

        def third(c):
            nc.vector.tensor_tensor(a[:, c], wc[:].indirect(lst(p3, c)), ne[:, c], ALU.subtract)

        def addsig(dst, s, src, c):
            nc.vector.scalar_tensor_tensor(dst[:, c], s[:, c], kap2[:], src[:, c], ALU.mult, ALU.add)

        def mkbase(c):
            nc.vector.scalar_tensor_tensor(base[:, c], mu[:, c], -3.0, con[:, c], ALU.mult, ALU.add)

        def fetch(dst, p, src, c):
            nc.vector.tensor_tensor(dst[:, c], mu[:].indirect(lst(p, c)), src[:, c], ALU.add)

        tanh(0)
        dbl_v(0)
        tanh(1)
        dbl_v(1)
        square(Q[0])
        tanh(2)
        scaled(H[0])
        square(Q[1])
        dbl_v(2)
        scaled(Q[2])
        square_v(Q[2])
        tanh(3)
        dbl_a(3)
        square(Q[3])
        well(Q[2])
        scaled(Q[3])
        well(H[0])
        well(Q[3])
        sig(s1, p1, H[0])
        sig(s1, p1, H[1])
        sig(s2, p2, H[0])
        sig(s2, p2, H[1])
        third(H[0])
        third(H[1])
        addsig(b, s1, a, H[0])
        addsig(b, s1, a, H[1])
        addsig(mu, s2, b, H[0])
        addsig(mu, s2, b, H[1])
        mkbase(H[0])
        mkbase(H[1])
        for dst, p, src in ((t1, p1, base), (t2, p2, t1), (t3, p3, t2)):
            for h in H:
                fetch(dst, p, src, h)
        for h in H:
            nc.sync.dma_start(out[:, h], t3[:, h])
